import numpy as np
import ml_dtypes

BF16 = ml_dtypes.bfloat16


def bf(x):
    return np.asarray(x, np.float32).astype(BF16)


def f32(x):
    return np.asarray(x, np.float32)


def f64(x):
    return np.asarray(x).astype(np.float64)


def striped(idx):
    return np.tile(idx.reshape(-1, 16).T, (8, 1))


def rows(idx, k):
    return np.tile(idx, (k, 1))


def look(tab, idx):
    return np.take_along_axis(f64(tab), rows(idx, len(tab)), axis=1)


K, S, D, V, N, M = 128, 2048, 2, 512, 1024, 128


def setup_inputs():
    return {"tab": f32(np.random.standard_normal((K, S))), "u0": f32(np.random.uniform(0.2, 1.0, (K, V))), "u1": f32(np.random.uniform(0.2, 1.0, (K, V))), "w": bf(np.random.standard_normal((K, M)) / np.sqrt(K)), "b": f32(0.5 * np.random.standard_normal((M, 1))), "offs": striped(np.random.permutation(S)[:N])}


def reference(tab, u0, u1, w, b, offs):
    idx = offs[:16].T.reshape(-1)
    x = f64(u0) * np.minimum(np.maximum(look(tab, idx[:V]), -1.25), 1.0) + f64(u1) * np.minimum(np.maximum(look(tab, idx[1 * V:2 * V]), -1.25), 1.0)
    return np.maximum(f64(w).T @ x + f64(b), 0.0)

@@ -1,0 +1,48 @@
+import concourse.mybir as mybir
+
+F32, BF16, U16 = mybir.dt.float32, mybir.dt.bfloat16, mybir.dt.uint16
+ALU = mybir.AluOpType
+RELU = mybir.ActivationFunctionType.Relu
+
+P = 128
+T = 2048
+V = 512
+LANES = 16
+LOW, HIGH = -1.25, 1.0
+
+FLOPS = 2 * P * P * V
+
+
+def tile_lookup_clipmix_relu_kernel(tc, tab, u0, u1, w, b, offs, out):
+    nc = tc.nc
+    columns = V // LANES
+    with tc.tile_pool(name="held", bufs=1) as held, tc.psum_pool(name="psum", bufs=1) as psum:
+        offsets = held.tile([P, 2 * columns], U16)
+        table = held.tile([P, T], F32)
+        weight0 = held.tile([P, V], F32)
+        weight1 = held.tile([P, V], F32)
+        layer = held.tile([P, P], BF16)
+        bias = held.tile([P, 1], F32)
+        nc.sync.dma_start(offsets[:], offs)
+        nc.sync.dma_start(table[:], tab)
+        nc.sync.dma_start(weight0[:], u0)
+        nc.sync.dma_start(weight1[:], u1)
+        nc.sync.dma_start(layer[:], w)
+        nc.sync.dma_start(bias[:], b)
+
+        clamped0 = held.tile([P, V], F32)
+        clamped1 = held.tile([P, V], F32)
+        product0 = held.tile([P, V], F32)
+        product1 = held.tile([P, V], F32)
+        x = held.tile([P, V], BF16)
+        nc.vector.tensor_scalar(clamped0[:], table[:].indirect(offsets[:, 0:columns]), LOW, HIGH, ALU.max, ALU.min)
+        nc.vector.tensor_scalar(clamped1[:], table[:].indirect(offsets[:, columns : 2 * columns]), LOW, HIGH, ALU.max, ALU.min)
+        nc.vector.tensor_tensor(product0[:], clamped0[:], weight0[:], ALU.mult)
+        nc.vector.tensor_tensor(product1[:], clamped1[:], weight1[:], ALU.mult)
+        nc.vector.tensor_tensor(x[:], product0[:], product1[:], ALU.add)
+
+        total = psum.tile([P, V], F32)
+        nc.tensor.matmul(total[:], layer[:], x[:], start=True, stop=True)
+        result = held.tile([P, V], F32)
+        nc.scalar.activation(result[:], total[:], RELU, bias=bias[:])
+        nc.sync.dma_start(out, result[:])

@@ -8,6 +8,7 @@ P = 128
 T = 2048
 V = 512
 LANES = 16
+HALF = V // 2
 LOW, HIGH = -1.25, 1.0
 
 FLOPS = 2 * P * P * V
@@ -19,30 +20,29 @@ def tile_lookup_clipmix_relu_kernel(tc, tab, u0, u1, w, b, offs, out):
     with tc.tile_pool(name="held", bufs=1) as held, tc.psum_pool(name="psum", bufs=1) as psum:
         offsets = held.tile([P, 2 * columns], U16)
         table = held.tile([P, T], F32)
-        weight0 = held.tile([P, V], F32)
-        weight1 = held.tile([P, V], F32)
+        weights = held.tile([P, 2, V], F32)
         layer = held.tile([P, P], BF16)
         bias = held.tile([P, 1], F32)
         nc.sync.dma_start(offsets[:], offs)
         nc.sync.dma_start(table[:], tab)
-        nc.sync.dma_start(weight0[:], u0)
-        nc.sync.dma_start(weight1[:], u1)
+        nc.sync.dma_start(weights[:, 0, :], u0)
+        nc.sync.dma_start(weights[:, 1, :], u1)
         nc.sync.dma_start(layer[:], w)
         nc.sync.dma_start(bias[:], b)
 
-        clamped0 = held.tile([P, V], F32)
-        clamped1 = held.tile([P, V], F32)
-        product0 = held.tile([P, V], F32)
-        product1 = held.tile([P, V], F32)
+        clamped = held.tile([P, 2, V], F32)
+        products = held.tile([P, 2, V], F32)
         x = held.tile([P, V], BF16)
-        nc.vector.tensor_scalar(clamped0[:], table[:].indirect(offsets[:, 0:columns]), LOW, HIGH, ALU.max, ALU.min)
-        nc.vector.tensor_scalar(clamped1[:], table[:].indirect(offsets[:, columns : 2 * columns]), LOW, HIGH, ALU.max, ALU.min)
-        nc.vector.tensor_tensor(product0[:], clamped0[:], weight0[:], ALU.mult)
-        nc.vector.tensor_tensor(product1[:], clamped1[:], weight1[:], ALU.mult)
-        nc.vector.tensor_tensor(x[:], product0[:], product1[:], ALU.add)
-
-        total = psum.tile([P, V], F32)
-        nc.tensor.matmul(total[:], layer[:], x[:], start=True, stop=True)
         result = held.tile([P, V], F32)
-        nc.scalar.activation(result[:], total[:], RELU, bias=bias[:])
-        nc.sync.dma_start(out, result[:])
+        for half in range(2):
+            here = slice(half * HALF, (half + 1) * HALF)
+            for k in range(2):
+                first = (k * V + half * HALF) // LANES
+                picked = table[:].indirect(offsets[:, first : first + HALF // LANES])
+                nc.vector.tensor_scalar(clamped[:, k, here], picked, LOW, HIGH, ALU.max, ALU.min)
+            nc.vector.tensor_tensor(products[:, :, here], clamped[:, :, here], weights[:, :, here], ALU.mult)
+            nc.vector.tensor_tensor(x[:, here], products[:, 0, here], products[:, 1, here], ALU.add)
+            total = psum.tile([P, HALF], F32, name=f"total{half}")
+            nc.tensor.matmul(total[:], layer[:], x[:, here], start=True, stop=True)
+            nc.scalar.activation(result[:, here], total[:], RELU, bias=bias[:])
+            nc.sync.dma_start(out[:, here], result[:, here])

@@ -34,13 +34,14 @@ def tile_lookup_clipmix_relu_kernel(tc, tab, u0, u1, w, b, offs, out):
         products = held.tile([P, 2, V], F32)
         x = held.tile([P, V], BF16)
         result = held.tile([P, V], F32)
-        for half in range(2):
-            here = slice(half * HALF, (half + 1) * HALF)
-            for k in range(2):
+        halves = [slice(0, HALF), slice(HALF, V)]
+        for k, engine in enumerate((nc.gpsimd, nc.vector)):
+            for half, here in enumerate(halves):
                 first = (k * V + half * HALF) // LANES
                 picked = table[:].indirect(offsets[:, first : first + HALF // LANES])
                 nc.vector.tensor_scalar(clamped[:, k, here], picked, LOW, HIGH, ALU.max, ALU.min)
-            nc.vector.tensor_tensor(products[:, :, here], clamped[:, :, here], weights[:, :, here], ALU.mult)
+                engine.tensor_tensor(products[:, k, here], clamped[:, k, here], weights[:, k, here], ALU.mult)
+        for half, here in enumerate(halves):
             nc.vector.tensor_tensor(x[:, here], products[:, 0, here], products[:, 1, here], ALU.add)
             total = psum.tile([P, HALF], F32, name=f"total{half}")
             nc.tensor.matmul(total[:], layer[:], x[:, here], start=True, stop=True)

import concourse.mybir as mybir

F32, BF16, U16 = mybir.dt.float32, mybir.dt.bfloat16, mybir.dt.uint16
ALU = mybir.AluOpType
RELU = mybir.ActivationFunctionType.Relu

P = 128
T = 2048
V = 512
LANES = 16
HALF = V // 2
LOW, HIGH = -1.25, 1.0

FLOPS = 2 * P * P * V


def tile_lookup_clipmix_relu_kernel(tc, tab, u0, u1, w, b, offs, out):
    nc = tc.nc
    columns = V // LANES
    with tc.tile_pool(name="held", bufs=1) as held, tc.psum_pool(name="psum", bufs=1) as psum:
        offsets = held.tile([P, 2 * columns], U16)
        table = held.tile([P, T], F32)
        weights = held.tile([P, 2, V], F32)
        layer = held.tile([P, P], BF16)
        bias = held.tile([P, 1], F32)
        nc.sync.dma_start(offsets[:], offs)
        nc.sync.dma_start(table[:], tab)
        nc.sync.dma_start(weights[:, 0, :], u0)
        nc.sync.dma_start(weights[:, 1, :], u1)
        nc.sync.dma_start(layer[:], w)
        nc.sync.dma_start(bias[:], b)

        clamped = held.tile([P, 2, V], F32)
        products = held.tile([P, 2, V], F32)
        x = held.tile([P, V], BF16)
        result = held.tile([P, V], F32)
        halves = [slice(0, HALF), slice(HALF, V)]
        for k, engine in enumerate((nc.gpsimd, nc.vector)):
            for half, here in enumerate(halves):
                first = (k * V + half * HALF) // LANES
                picked = table[:].indirect(offsets[:, first : first + HALF // LANES])
                nc.vector.tensor_scalar(clamped[:, k, here], picked, LOW, HIGH, ALU.max, ALU.min)
                engine.tensor_tensor(products[:, k, here], clamped[:, k, here], weights[:, k, here], ALU.mult)
        for half, here in enumerate(halves):
            nc.vector.tensor_tensor(x[:, here], products[:, 0, here], products[:, 1, here], ALU.add)
            total = psum.tile([P, HALF], F32, name=f"total{half}")
            nc.tensor.matmul(total[:], layer[:], x[:, here], start=True, stop=True)
            nc.scalar.activation(result[:, here], total[:], RELU, bias=bias[:])
            nc.sync.dma_start(out[:, here], result[:, here])
